import numpy as np
import ml_dtypes


def mxq(x, axis, fmt="e4m3"):
    dtype, down = {"e4m3": (ml_dtypes.float8_e4m3fn, 7), "e5m2": (ml_dtypes.float8_e5m2, 14)}[fmt]
    v = np.moveaxis(np.asarray(x, np.float32).astype(ml_dtypes.bfloat16).astype(np.float64), axis, -1)
    blocks = v.reshape(v.shape[:-1] + (-1, 32))
    amax = np.abs(blocks).max(-1, keepdims=True)
    byte = np.maximum(np.where(amax > 0, np.frexp(amax)[1] - 1 + 127, 0) - down, 1)
    scale = np.exp2(byte - 127.0)
    codes = (blocks / scale).astype(np.float32).astype(dtype).astype(np.float64)
    return np.moveaxis((codes * scale).reshape(v.shape), -1, axis)


WIDE = False


def mx_kscale(k):
    if not WIDE:
        return np.ones(k)
    levels = np.array([10, -10, 5, -5, 0])
    if k % 512:
        return np.exp2(np.random.permutation(np.resize(levels, k // 32))).repeat(32)
    a = np.empty((k // 512, 16))
    for p in range(k // 512):
        a[p, :8] = np.random.permutation(np.resize(levels, 8))
        for g in range(8):
            far = levels[np.abs(levels - a[p, g]) >= 10]
            a[p, g + 8] = far[np.random.randint(len(far))]
    return np.exp2(a.ravel()).repeat(32)


def f64(x):
    return np.asarray(x).astype(np.float64)


def striped(idx):
    return np.tile(np.asarray(idx).reshape(-1, 16).T, (8, 1)).astype(np.uint16)


def unstriped(offs):
    return offs[:16].T.reshape(-1).astype(np.int64)


E2M1 = np.array([0.0, 0.5, 1.0, 1.5, 2.0, 3.0, 4.0, 6.0, -0.0, -0.5, -1.0, -1.5, -2.0, -3.0, -4.0, -6.0])


def pack_weight(w, fmt):
    k, n = w.shape
    w = f64(np.asarray(w, np.float32).astype(ml_dtypes.bfloat16)).reshape(k // 32, 32, n)
    amax = np.abs(w).max(1)
    if fmt == "e4m3":
        byte = np.frexp(amax)[1] - 1 + 127 - 7
    else:
        mant, ex = np.frexp(amax / 6.0)
        byte = np.where(mant > 0.5, ex, ex - 1) + 127
    byte = np.clip(np.where(amax > 0, byte, 1), 1, 254)
    scaled = (w * np.exp2(127.0 - byte)[:, None, :]).reshape(k, n).astype(np.float32)
    by_word = np.ascontiguousarray(scaled.reshape(k // 512, 128, 4, n).transpose(0, 1, 3, 2))
    if fmt == "e4m3":
        words = by_word.astype(ml_dtypes.float8_e4m3fn).view(np.uint8)
    else:
        c = by_word.astype(ml_dtypes.float4_e2m1fn).view(np.uint8) & 0xF
        words = (c[..., 0::2] | (c[..., 1::2] << 4)).reshape(k // 512, 128, 2 * n)
    return np.ascontiguousarray(words), np.ascontiguousarray(byte.astype(np.uint8).reshape(k // 512, 16, n))


def unpack_weight(words, scales, fmt):
    g, _, n = scales.shape
    words = np.ascontiguousarray(words).reshape(g, 128, n, -1)
    if fmt == "e4m3":
        vals = words.view(ml_dtypes.float8_e4m3fn).astype(np.float64)
    else:
        nib = np.empty((g, 128, n, 4), np.uint8)
        nib[..., 0::2] = words & 0xF
        nib[..., 1::2] = words >> 4
        vals = E2M1[nib]
    vals = vals * np.repeat(np.exp2(scales.astype(np.float64) - 127.0), 8, axis=1)[..., None]
    return vals.transpose(0, 1, 3, 2).reshape(g * 512, n)


def sigmoid(v):
    return 1.0 / (1.0 + np.exp(-v))


D, E, T, I, Q = 512, 512, 2048, 512, 128


def setup_inputs():
    n = np.random.standard_normal
    idx = np.random.permutation(T)[:I]
    idx2 = np.random.permutation(I)[:I]
    fd = mx_kscale(D)
    fe = mx_kscale(E)
    keysp = pack_weight(n((D, T)) / fd[:, None], "e4m3")
    valsp = pack_weight(n((E, T)) / fe[:, None], "e4m3")
    return {
        "query": (n((D, Q)) * 0.7 / np.sqrt(D) * fd[:, None]).astype(np.float32),
        "lam": (np.random.uniform(0.5, 2.0, (Q, 1))).astype(np.float32),
        "keys_words": keysp[0],
        "keys_scales": keysp[1],
        "gout": (n((E, Q)) * 1 / np.sqrt(E) * fe[:, None]).astype(np.float32),
        "vals_words": valsp[0],
        "vals_scales": valsp[1],
        "size": (np.random.uniform(0.5, 2.0, (1, I))).astype(np.float32),
        "old": (0.5 * n((Q, T))).astype(np.float32),
        "offs": striped(idx),
        "offs2": striped(idx2),
    }


def reference(query, lam, keys_words, keys_scales, gout, vals_words, vals_scales, size, old, offs, offs2):
    idx = unstriped(offs)
    idx2 = unstriped(offs2)
    keysu = unpack_weight(keys_words, keys_scales, "e4m3")
    valsu = unpack_weight(vals_words, vals_scales, "e4m3")
    queryq = mxq(f64(query), 0, "e4m3")
    keysidxg = keysu[:, idx]
    a = queryq.T @ keysidxg
    b = sigmoid(a)
    s = a + b[:, idx2] * f64(lam)
    p = np.exp(s - np.max(s, axis=1, keepdims=True))
    z = np.sum(p, axis=1, keepdims=True)
    goutq = mxq(f64(gout), 0, "e4m3")
    valsidxg = valsu[:, idx]
    c0 = goutq.T @ valsidxg
    dz = np.sum(c0 * p * f64(size) / np.square(z) * (-1.0), axis=1, keepdims=True)
    dp = c0 / z * f64(size) + dz
    ds = dp * p
    e1 = ds * f64(lam)
    s1 = np.zeros((Q, I))
    s1[:, idx2] = e1
    da = ds + s1 * b * (1.0 - b)
    gs = da * 512.0
    gf = np.zeros((Q, T))
    gf[:, idx] = gs
    y = f64(old) + gf
    return y

@@ -1,0 +1,197 @@
+from contextlib import ExitStack
+
+import concourse.mybir as mybir
+from concourse.masks import make_identity
+
+D, E, T, I, Q = 512, 512, 2048, 512, 128
+FLOPS = 2 * Q * I * (D + E)
+
+F32 = mybir.dt.float32
+BF16 = mybir.dt.bfloat16
+I32 = mybir.dt.int32
+U32 = mybir.dt.uint32
+U16 = mybir.dt.uint16
+U8 = mybir.dt.uint8
+FP8X4 = mybir.dt.float8_e4m3fn_x4
+ALU = mybir.AluOpType
+ACT = mybir.ActivationFunctionType
+AXIS = mybir.AxisListType
+
+P = 128
+PACK = 4
+HALF = I // 2
+SLOT_WINDOW = 704
+GRAD_SCALE = 512.0
+STORE_WIDTHS = (256, 512, 512, 512, 256)
+
+
+def load_words(nc, tile, words):
+    nc.sync.dma_start(out=tile[:], in_=words[0].rearrange("p n t -> p (n t)").bitcast(I32))
+
+
+def load_scale_rows(queues, tile, scales):
+    for quad in range(4):
+        queues[quad].dma_start(
+            out=tile[32 * quad : 32 * quad + 4, :].bitcast(I32),
+            in_=scales[0, 4 * quad : 4 * quad + 4, :].bitcast(I32),
+        )
+
+
+def tile_attend_blinked_s_kernel(
+    tc, query, lam, keys_words, keys_scales, gout, vals_words, vals_scales, size, old, offs, offs2, out
+):
+    nc = tc.nc
+    halves = [slice(h * HALF, (h + 1) * HALF) for h in range(2)]
+    list_halves = [slice(h * HALF // 16, (h + 1) * HALF // 16) for h in range(2)]
+
+    with ExitStack() as ctx:
+        sb = ctx.enter_context(tc.tile_pool(name="sb", bufs=1))
+        ps = ctx.enter_context(tc.psum_pool(name="ps", bufs=1))
+
+        token_list = sb.tile([P, I // 16], U16)
+        link_list = sb.tile([P, I // 16], U16)
+        key_scale_pool = sb.tile([P, T], U8, align_bytes=64, tag="key_scales_then_gout")
+        val_scale_pool = sb.tile([P, T], U8, align_bytes=64, tag="val_scales_then_linked")
+        query_raw = sb.tile([P, PACK, Q], F32)
+
+        ident = sb.tile([P, P], F32)
+        make_identity(nc, ident[:])
+        size_cols = sb.tile([P, PACK], F32)
+        lam_col = sb.tile([P, 1], F32)
+        nc.gpsimd.dma_start(out=size_cols[:], in_=size.rearrange("o (p t) -> p (o t)", t=PACK))
+        nc.gpsimd.dma_start(out=lam_col[:], in_=lam)
+        nc.vector.memset(key_scale_pool[:].bitcast(I32), 0)
+        nc.vector.memset(val_scale_pool[:].bitcast(I32), 0)
+
+        nc.sync.dma_start(out=token_list[:], in_=offs)
+        nc.sync.dma_start(out=link_list[:], in_=offs2)
+        nc.sync.dma_start(out=query_raw[:], in_=query.rearrange("(p j) w -> p j w", j=PACK))
+        load_scale_rows([nc.scalar] * 4, key_scale_pool, keys_scales)
+        key_pool = sb.tile([P, T], I32, align_bytes=64, tag="keys_then_val_scales")
+        load_words(nc, key_pool, keys_words)
+        val_pool = sb.tile([P, T], I32, align_bytes=64, tag="vals_then_old")
+        load_words(nc, val_pool, vals_words)
+        load_scale_rows([nc.scalar, nc.scalar, nc.gpsimd, nc.gpsimd], val_scale_pool, vals_scales)
+
+        token_grad = sb.tile([P, T], F32)
+        spare_in = sb.tile([P, SLOT_WINDOW - I], F32)
+        nc.vector.memset(spare_in[:], 0.0)
+        nc.vector.memset(token_grad[:], 0.0)
+        sig = sb.tile([P, SLOT_WINDOW], F32, align_bytes=64, tag="sig_then_val_codes")
+        nc.scalar.activation(sig[:, I:], spare_in[:], ACT.Sigmoid)
+        link_grad = sb.tile([P, SLOT_WINDOW], F32)
+
+        query_bf = sb.tile([P, Q, PACK], BF16, align_bytes=64)
+        query_codes = sb.tile([P, Q], U32, align_bytes=64, tag="row_codes")
+        query_scales = sb.tile([P, Q], U8, align_bytes=64, tag="row_scales")
+        nc.vector.tensor_copy(out=query_bf[:], in_=query_raw[:].rearrange("p j w -> p w j"))
+        key_scales = sb.tile([P, I], U8, align_bytes=64)
+        nc.vector.tensor_copy(key_scales[:], key_scale_pool[:].indirect(token_list[:]))
+        nc.vector.quantize_mx(
+            out=query_codes[:].bitcast(FP8X4), scales=query_scales[:], in_=query_bf[:].rearrange("p w j -> p (w j)")
+        )
+
+        size_ps = ps.tile([P, PACK, P], F32)
+        for t in range(PACK):
+            nc.tensor.transpose(size_ps[:, t, :], size_cols[:, t : t + 1].to_broadcast([P, P]), ident[:])
+        size_row = sb.tile([P, P, PACK], F32)
+        nc.scalar.copy(size_row[:], size_ps[:].rearrange("p t n -> p n t"))
+        size_flat = size_row[:].rearrange("p n t -> p (n t)")
+
+        gout_raw = sb.tile([P, PACK, Q], F32, align_bytes=64, tag="key_scales_then_gout")
+        nc.scalar.dma_start(out=gout_raw[:], in_=gout.rearrange("(p j) w -> p j w", j=PACK))
+
+        base = sb.tile([P, 3], F32)
+        nc.gpsimd.memset(base[:, 2:3], GRAD_SCALE)
+        nc.gpsimd.tensor_scalar(base[:, 0:1], lam_col[:], -GRAD_SCALE, 0.0, ALU.mult, ALU.add)
+        nc.gpsimd.tensor_scalar(base[:, 1:2], lam_col[:], GRAD_SCALE / 4, 0.0, ALU.mult, ALU.add)
+
+        key_codes = sb.tile([P, I], U32, align_bytes=64, tag="key_codes_then_gout_bf")
+        score_ps = [ps.tile([P, HALF], F32, name=f"score_ps{h}") for h in range(2)]
+        for h in range(2):
+            nc.vector.tensor_copy(key_codes[:, halves[h]], key_pool[:].bitcast(U32).indirect(token_list[:, list_halves[h]]))
+            nc.tensor.matmul_mx(
+                out=score_ps[h][:],
+                lhsT=query_codes[:].bitcast(FP8X4),
+                lhsT_scale=query_scales[:],
+                rhs=key_codes[:, halves[h]].bitcast(FP8X4),
+                rhs_scale=key_scales[:, halves[h]],
+                start=True,
+                stop=True,
+            )
+            nc.scalar.activation(sig[:, halves[h]], score_ps[h][:], ACT.Sigmoid)
+
+        gout_bf = sb.tile([P, Q, PACK], BF16, align_bytes=64, tag="key_codes_then_gout_bf")
+        gout_codes = sb.tile([P, Q], U32, align_bytes=64, tag="row_codes")
+        gout_scales = sb.tile([P, Q], U8, align_bytes=64, tag="row_scales")
+        nc.scalar.copy(gout_bf[:], gout_raw[:].rearrange("p j w -> p w j"))
+        val_scales = sb.tile([P, I], U8, align_bytes=64, tag="keys_then_val_scales")
+        nc.vector.tensor_copy(val_scales[:], val_scale_pool[:].indirect(token_list[:]))
+
+        linked = sb.tile([P, I], F32, align_bytes=64, tag="val_scales_then_linked")
+        nc.vector.tensor_copy(linked[:], sig[:].indirect(link_list[:]))
+        logits = sb.tile([P, I], F32)
+        for h in range(2):
+            nc.vector.scalar_tensor_tensor(
+                logits[:, halves[h]], linked[:, halves[h]], lam_col[:], score_ps[h][:], ALU.mult, ALU.add
+            )
+
+        nc.vector.quantize_mx(
+            out=gout_codes[:].bitcast(FP8X4), scales=gout_scales[:], in_=gout_bf[:].rearrange("p w j -> p (w j)")
+        )
+        val_codes = sb.tile([P, I], U32, align_bytes=64, tag="sig_then_val_codes")
+        dot_ps = [ps.tile([P, HALF], F32, name=f"dot_ps{h}") for h in range(2)]
+        weighted = sb.tile([P, I], F32)
+
+        def gather_values(h):
+            nc.vector.tensor_copy(val_codes[:, halves[h]], val_pool[:].bitcast(U32).indirect(token_list[:, list_halves[h]]))
+            nc.tensor.matmul_mx(
+                out=dot_ps[h][:],
+                lhsT=gout_codes[:].bitcast(FP8X4),
+                lhsT_scale=gout_scales[:],
+                rhs=val_codes[:, halves[h]].bitcast(FP8X4),
+                rhs_scale=val_scales[:, halves[h]],
+                start=True,
+                stop=True,
+            )
+
+        neg_max = sb.tile([P, 1], F32)
+        nc.vector.tensor_reduce(neg_max[:], logits[:], AXIS.X, ALU.max, negate=True)
+        expo = sb.tile([P, I], F32)
+        row_sum = sb.tile([P, 1], F32)
+        nc.scalar.activation(expo[:], logits[:], ACT.Exp, bias=neg_max[:], accum_out=row_sum[:])
+        gather_values(0)
+        gather_values(1)
+        old_sb = sb.tile([P, T], F32, align_bytes=64, tag="vals_then_old")
+        nc.sync.dma_start(out=old_sb[:], in_=old)
+        inv_sum = sb.tile([P, 1], F32)
+        nc.vector.reciprocal(inv_sum[:], row_sum[:])
+        for h in range(2):
+            nc.vector.tensor_tensor(weighted[:, halves[h]], dot_ps[h][:], size_flat[:, halves[h]], ALU.mult)
+
+        nc.scalar.activation(logits[:], linked[:], ACT.Square, bias=-0.5)
+
+        products = sb.tile([P, I], F32)
+        mean = sb.tile([P, 1], F32)
+        nc.vector.scalar_tensor_tensor(
+            products[:], expo[:], inv_sum[:], weighted[:], ALU.mult, ALU.mult, accum_out=mean[:]
+        )
+        coef = sb.tile([P, 3], F32)
+        nc.vector.tensor_scalar(coef[:], base[:], inv_sum[:], None, ALU.mult)
+        raw_grad = sb.tile([P, I], F32)
+        nc.vector.scalar_tensor_tensor(raw_grad[:], weighted[:], mean[:], expo[:], ALU.subtract, ALU.mult)
+        link_factor = sb.tile([P, I], F32)
+        nc.scalar.activation(link_factor[:], logits[:], ACT.Identity, bias=coef[:, 1:2], scale=coef[:, 0:1])
+        nc.vector.tensor_tensor(link_grad[:].indirect(link_list[:]), raw_grad[:], link_factor[:], ALU.mult)
+        own_grad = sb.tile([P, I], F32)
+        nc.scalar.activation(own_grad[:], raw_grad[:], ACT.Copy, scale=coef[:, 2:3])
+        nc.vector.tensor_tensor(token_grad[:].indirect(token_list[:]), link_grad[:, :I], own_grad[:], ALU.add)
+
+        start = 0
+        for n, width in enumerate(STORE_WIDTHS):
+            cols = slice(start, start + width)
+            result = sb.tile([P, width], F32, name=f"result{n}")
+            nc.vector.tensor_tensor(result[:], old_sb[:, cols], token_grad[:, cols], ALU.add)
+            queue = nc.sync if n % 2 == 0 else nc.scalar
+            queue.dma_start(out=out[:, cols], in_=result[:])
+            start = start + width

@@ -29,9 +29,9 @@ def load_words(nc, tile, words):
     nc.sync.dma_start(out=tile[:], in_=words[0].rearrange("p n t -> p (n t)").bitcast(I32))
 
 
-def load_scale_rows(queues, tile, scales):
+def load_scale_rows(nc, tile, scales):
     for quad in range(4):
-        queues[quad].dma_start(
+        nc.sync.dma_start(
             out=tile[32 * quad : 32 * quad + 4, :].bitcast(I32),
             in_=scales[0, 4 * quad : 4 * quad + 4, :].bitcast(I32),
         )
@@ -50,46 +50,45 @@ def tile_attend_blinked_s_kernel(
 
         token_list = sb.tile([P, I // 16], U16)
         link_list = sb.tile([P, I // 16], U16)
-        key_scale_pool = sb.tile([P, T], U8, align_bytes=64, tag="key_scales_then_gout")
-        val_scale_pool = sb.tile([P, T], U8, align_bytes=64, tag="val_scales_then_linked")
+        key_scale_pool = sb.tile([P, T], U8, align_bytes=64, tag="key_scales_then_val_codes")
         query_raw = sb.tile([P, PACK, Q], F32)
+        key_pool = sb.tile([P, T], I32, align_bytes=64, tag="keys_then_scales")
+        nc.vector.memset(key_scale_pool[:].bitcast(I32), 0)
+        size_cols = sb.tile([P, PACK], F32)
+        nc.sync.dma_start(out=token_list[:], in_=offs)
+        nc.scalar.dma_start(out=size_cols[:], in_=size.rearrange("o (p t) -> p (o t)", t=PACK))
+        nc.sync.dma_start(out=link_list[:], in_=offs2)
+        load_words(nc, key_pool, keys_words)
+        nc.sync.dma_start(out=query_raw[:], in_=query.rearrange("(p j) w -> p j w", j=PACK))
+        load_scale_rows(nc, key_scale_pool, keys_scales)
 
         ident = sb.tile([P, P], F32)
         make_identity(nc, ident[:])
-        size_cols = sb.tile([P, PACK], F32)
-        lam_col = sb.tile([P, 1], F32)
-        nc.gpsimd.dma_start(out=size_cols[:], in_=size.rearrange("o (p t) -> p (o t)", t=PACK))
-        nc.gpsimd.dma_start(out=lam_col[:], in_=lam)
-        nc.vector.memset(key_scale_pool[:].bitcast(I32), 0)
-        nc.vector.memset(val_scale_pool[:].bitcast(I32), 0)
 
-        nc.sync.dma_start(out=token_list[:], in_=offs)
-        nc.sync.dma_start(out=link_list[:], in_=offs2)
-        nc.sync.dma_start(out=query_raw[:], in_=query.rearrange("(p j) w -> p j w", j=PACK))
-        load_scale_rows([nc.scalar] * 4, key_scale_pool, keys_scales)
-        key_pool = sb.tile([P, T], I32, align_bytes=64, tag="keys_then_val_scales")
-        load_words(nc, key_pool, keys_words)
-        val_pool = sb.tile([P, T], I32, align_bytes=64, tag="vals_then_old")
+        sig = sb.tile([P, SLOT_WINDOW], F32, align_bytes=64, tag="sig_then_val_scales")
+        late = ctx.enter_context(tc.tile_pool(name="late", bufs=1))
+        spare_in = late.tile([P, SLOT_WINDOW - I], F32, offset=1792)
+        nc.vector.memset(spare_in[:], 0.0)
+        nc.scalar.activation(sig[:, I:], spare_in[:], ACT.Sigmoid)
+        gout_raw = late.tile([P, PACK, Q], F32, offset=0)
+        lam_col = late.tile([P, 1], F32, offset=2080)
+        val_pool = late.tile([P, T], I32, align_bytes=64, tag="vals_then_old", offset=2112)
         load_words(nc, val_pool, vals_words)
-        load_scale_rows([nc.scalar, nc.scalar, nc.gpsimd, nc.gpsimd], val_scale_pool, vals_scales)
+        nc.sync.dma_start(out=gout_raw[:], in_=gout.rearrange("(p j) w -> p j w", j=PACK))
+        nc.sync.dma_start(out=lam_col[:], in_=lam)
 
         token_grad = sb.tile([P, T], F32)
-        spare_in = sb.tile([P, SLOT_WINDOW - I], F32)
-        nc.vector.memset(spare_in[:], 0.0)
         nc.vector.memset(token_grad[:], 0.0)
-        sig = sb.tile([P, SLOT_WINDOW], F32, align_bytes=64, tag="sig_then_val_codes")
-        nc.scalar.activation(sig[:, I:], spare_in[:], ACT.Sigmoid)
         link_grad = sb.tile([P, SLOT_WINDOW], F32)
 
         query_bf = sb.tile([P, Q, PACK], BF16, align_bytes=64)
         query_codes = sb.tile([P, Q], U32, align_bytes=64, tag="row_codes")
         query_scales = sb.tile([P, Q], U8, align_bytes=64, tag="row_scales")
-        nc.vector.tensor_copy(out=query_bf[:], in_=query_raw[:].rearrange("p j w -> p w j"))
-        key_scales = sb.tile([P, I], U8, align_bytes=64)
-        nc.vector.tensor_copy(key_scales[:], key_scale_pool[:].indirect(token_list[:]))
-        nc.vector.quantize_mx(
-            out=query_codes[:].bitcast(FP8X4), scales=query_scales[:], in_=query_bf[:].rearrange("p w j -> p (w j)")
-        )
+        nc.scalar.copy(query_bf[:], query_raw[:].rearrange("p j w -> p w j"))
+
+        val_scale_pool = sb.tile([P, T], U8, align_bytes=64)
+        nc.vector.memset(val_scale_pool[:].bitcast(I32), 0)
+        load_scale_rows(nc, val_scale_pool, vals_scales)
 
         size_ps = ps.tile([P, PACK, P], F32)
         for t in range(PACK):
@@ -98,9 +97,6 @@ def tile_attend_blinked_s_kernel(
         nc.scalar.copy(size_row[:], size_ps[:].rearrange("p t n -> p n t"))
         size_flat = size_row[:].rearrange("p n t -> p (n t)")
 
-        gout_raw = sb.tile([P, PACK, Q], F32, align_bytes=64, tag="key_scales_then_gout")
-        nc.scalar.dma_start(out=gout_raw[:], in_=gout.rearrange("(p j) w -> p j w", j=PACK))
-
         base = sb.tile([P, 3], F32)
         nc.gpsimd.memset(base[:, 2:3], GRAD_SCALE)
         nc.gpsimd.tensor_scalar(base[:, 0:1], lam_col[:], -GRAD_SCALE, 0.0, ALU.mult, ALU.add)
@@ -108,8 +104,13 @@ def tile_attend_blinked_s_kernel(
 
         key_codes = sb.tile([P, I], U32, align_bytes=64, tag="key_codes_then_gout_bf")
         score_ps = [ps.tile([P, HALF], F32, name=f"score_ps{h}") for h in range(2)]
+        nc.vector.tensor_copy(key_codes[:], key_pool[:].bitcast(U32).indirect(token_list[:]))
+        nc.vector.quantize_mx(
+            out=query_codes[:].bitcast(FP8X4), scales=query_scales[:], in_=query_bf[:].rearrange("p w j -> p (w j)")
+        )
+        key_scales = sb.tile([P, I], U8, align_bytes=64, tag="keys_then_scales")
         for h in range(2):
-            nc.vector.tensor_copy(key_codes[:, halves[h]], key_pool[:].bitcast(U32).indirect(token_list[:, list_halves[h]]))
+            nc.vector.tensor_copy(key_scales[:, halves[h]], key_scale_pool[:].indirect(token_list[:, list_halves[h]]))
             nc.tensor.matmul_mx(
                 out=score_ps[h][:],
                 lhsT=query_codes[:].bitcast(FP8X4),
@@ -122,29 +123,25 @@ def tile_attend_blinked_s_kernel(
             nc.scalar.activation(sig[:, halves[h]], score_ps[h][:], ACT.Sigmoid)
 
         gout_bf = sb.tile([P, Q, PACK], BF16, align_bytes=64, tag="key_codes_then_gout_bf")
+        nc.scalar.copy(gout_bf[:], gout_raw[:].rearrange("p j w -> p w j"))
         gout_codes = sb.tile([P, Q], U32, align_bytes=64, tag="row_codes")
         gout_scales = sb.tile([P, Q], U8, align_bytes=64, tag="row_scales")
-        nc.scalar.copy(gout_bf[:], gout_raw[:].rearrange("p j w -> p w j"))
-        val_scales = sb.tile([P, I], U8, align_bytes=64, tag="keys_then_val_scales")
-        nc.vector.tensor_copy(val_scales[:], val_scale_pool[:].indirect(token_list[:]))
+        val_codes = sb.tile([P, I], U32, align_bytes=64, tag="key_scales_then_val_codes")
+        nc.vector.tensor_copy(val_codes[:], val_pool[:].bitcast(U32).indirect(token_list[:]))
+        old_sb = late.tile([P, T], F32, align_bytes=64, tag="vals_then_old", offset=2112)
+        nc.sync.dma_start(out=old_sb[:], in_=old)
 
-        linked = sb.tile([P, I], F32, align_bytes=64, tag="val_scales_then_linked")
+        linked = sb.tile([P, I], F32)
         nc.vector.tensor_copy(linked[:], sig[:].indirect(link_list[:]))
-        logits = sb.tile([P, I], F32)
-        for h in range(2):
-            nc.vector.scalar_tensor_tensor(
-                logits[:, halves[h]], linked[:, halves[h]], lam_col[:], score_ps[h][:], ALU.mult, ALU.add
-            )
-
         nc.vector.quantize_mx(
             out=gout_codes[:].bitcast(FP8X4), scales=gout_scales[:], in_=gout_bf[:].rearrange("p w j -> p (w j)")
         )
-        val_codes = sb.tile([P, I], U32, align_bytes=64, tag="sig_then_val_codes")
+        val_scales = sb.tile([P, I], U8, align_bytes=64, tag="sig_then_val_scales")
         dot_ps = [ps.tile([P, HALF], F32, name=f"dot_ps{h}") for h in range(2)]
         weighted = sb.tile([P, I], F32)
 
-        def gather_values(h):
-            nc.vector.tensor_copy(val_codes[:, halves[h]], val_pool[:].bitcast(U32).indirect(token_list[:, list_halves[h]]))
+        def value_dots(h):
+            nc.vector.tensor_copy(val_scales[:, halves[h]], val_scale_pool[:].indirect(token_list[:, list_halves[h]]))
             nc.tensor.matmul_mx(
                 out=dot_ps[h][:],
                 lhsT=gout_codes[:].bitcast(FP8X4),
@@ -155,22 +152,25 @@ def tile_attend_blinked_s_kernel(
                 stop=True,
             )
 
+        value_dots(0)
+        logits = sb.tile([P, I], F32)
+        for h in range(2):
+            nc.vector.scalar_tensor_tensor(
+                logits[:, halves[h]], linked[:, halves[h]], lam_col[:], score_ps[h][:], ALU.mult, ALU.add
+            )
         neg_max = sb.tile([P, 1], F32)
         nc.vector.tensor_reduce(neg_max[:], logits[:], AXIS.X, ALU.max, negate=True)
         expo = sb.tile([P, I], F32)
         row_sum = sb.tile([P, 1], F32)
         nc.scalar.activation(expo[:], logits[:], ACT.Exp, bias=neg_max[:], accum_out=row_sum[:])
-        gather_values(0)
-        gather_values(1)
-        old_sb = sb.tile([P, T], F32, align_bytes=64, tag="vals_then_old")
-        nc.sync.dma_start(out=old_sb[:], in_=old)
-        inv_sum = sb.tile([P, 1], F32)
-        nc.vector.reciprocal(inv_sum[:], row_sum[:])
+        value_dots(1)
         for h in range(2):
             nc.vector.tensor_tensor(weighted[:, halves[h]], dot_ps[h][:], size_flat[:, halves[h]], ALU.mult)
 
         nc.scalar.activation(logits[:], linked[:], ACT.Square, bias=-0.5)
 
+        inv_sum = sb.tile([P, 1], F32)
+        nc.vector.reciprocal(inv_sum[:], row_sum[:])
         products = sb.tile([P, I], F32)
         mean = sb.tile([P, 1], F32)
         nc.vector.scalar_tensor_tensor(

@@ -21,6 +21,7 @@ P = 128
 PACK = 4
 HALF = I // 2
 SLOT_WINDOW = 704
+SIG_SPARE = 560
 GRAD_SCALE = 512.0
 STORE_WIDTHS = (256, 512, 512, 512, 256)
 
@@ -29,9 +30,9 @@ def load_words(nc, tile, words):
     nc.sync.dma_start(out=tile[:], in_=words[0].rearrange("p n t -> p (n t)").bitcast(I32))
 
 
-def load_scale_rows(nc, tile, scales):
+def load_scale_rows(queue, tile, scales):
     for quad in range(4):
-        nc.sync.dma_start(
+        queue.dma_start(
             out=tile[32 * quad : 32 * quad + 4, :].bitcast(I32),
             in_=scales[0, 4 * quad : 4 * quad + 4, :].bitcast(I32),
         )
@@ -50,52 +51,49 @@ def tile_attend_blinked_s_kernel(
 
         token_list = sb.tile([P, I // 16], U16)
         link_list = sb.tile([P, I // 16], U16)
-        key_scale_pool = sb.tile([P, T], U8, align_bytes=64, tag="key_scales_then_val_codes")
+        key_scale_pool = sb.tile([P, T], U8, align_bytes=64)
         query_raw = sb.tile([P, PACK, Q], F32)
-        key_pool = sb.tile([P, T], I32, align_bytes=64, tag="keys_then_scales")
+        key_pool = sb.tile([P, T], I32, align_bytes=64)
         nc.vector.memset(key_scale_pool[:].bitcast(I32), 0)
-        size_cols = sb.tile([P, PACK], F32)
         nc.sync.dma_start(out=token_list[:], in_=offs)
-        nc.scalar.dma_start(out=size_cols[:], in_=size.rearrange("o (p t) -> p (o t)", t=PACK))
         nc.sync.dma_start(out=link_list[:], in_=offs2)
-        load_words(nc, key_pool, keys_words)
         nc.sync.dma_start(out=query_raw[:], in_=query.rearrange("(p j) w -> p j w", j=PACK))
-        load_scale_rows(nc, key_scale_pool, keys_scales)
+        load_words(nc, key_pool, keys_words)
+        load_scale_rows(nc.scalar, key_scale_pool, keys_scales)
 
         ident = sb.tile([P, P], F32)
         make_identity(nc, ident[:])
 
-        sig = sb.tile([P, SLOT_WINDOW], F32, align_bytes=64, tag="sig_then_val_scales")
+        sig = sb.tile([P, I + SIG_SPARE], F32, align_bytes=64, tag="sig_then_val_codes")
         late = ctx.enter_context(tc.tile_pool(name="late", bufs=1))
-        spare_in = late.tile([P, SLOT_WINDOW - I], F32, offset=1792)
+        spare_in = late.tile([P, SIG_SPARE], F32, offset=8128)
         nc.vector.memset(spare_in[:], 0.0)
         nc.scalar.activation(sig[:, I:], spare_in[:], ACT.Sigmoid)
-        gout_raw = late.tile([P, PACK, Q], F32, offset=0)
-        lam_col = late.tile([P, 1], F32, offset=2080)
-        val_pool = late.tile([P, T], I32, align_bytes=64, tag="vals_then_old", offset=2112)
+        val_scale_pool = late.tile([P, T], U8, align_bytes=64, offset=6144)
+        lam_col = late.tile([P, 1], F32, offset=8192)
+        size_cols = late.tile([P, PACK], F32, offset=8224)
+        gout_raw = late.tile([P, PACK, Q], F32, offset=8256)
+        val_pool = late.tile([P, T], I32, align_bytes=64, offset=10304)
         load_words(nc, val_pool, vals_words)
         nc.sync.dma_start(out=gout_raw[:], in_=gout.rearrange("(p j) w -> p j w", j=PACK))
         nc.sync.dma_start(out=lam_col[:], in_=lam)
+        nc.sync.dma_start(out=size_cols[:], in_=size.rearrange("o (p t) -> p (o t)", t=PACK))
 
         token_grad = sb.tile([P, T], F32)
         nc.vector.memset(token_grad[:], 0.0)
         link_grad = sb.tile([P, SLOT_WINDOW], F32)
+        nc.vector.memset(val_scale_pool[:].bitcast(I32), 0)
+        load_scale_rows(nc.sync, val_scale_pool, vals_scales)
 
         query_bf = sb.tile([P, Q, PACK], BF16, align_bytes=64)
-        query_codes = sb.tile([P, Q], U32, align_bytes=64, tag="row_codes")
-        query_scales = sb.tile([P, Q], U8, align_bytes=64, tag="row_scales")
+        query_codes = sb.tile([P, Q], U32, align_bytes=64)
+        query_scales = sb.tile([P, Q], U8, align_bytes=64)
         nc.scalar.copy(query_bf[:], query_raw[:].rearrange("p j w -> p w j"))
-
-        val_scale_pool = sb.tile([P, T], U8, align_bytes=64)
-        nc.vector.memset(val_scale_pool[:].bitcast(I32), 0)
-        load_scale_rows(nc, val_scale_pool, vals_scales)
-
-        size_ps = ps.tile([P, PACK, P], F32)
-        for t in range(PACK):
-            nc.tensor.transpose(size_ps[:, t, :], size_cols[:, t : t + 1].to_broadcast([P, P]), ident[:])
-        size_row = sb.tile([P, P, PACK], F32)
-        nc.scalar.copy(size_row[:], size_ps[:].rearrange("p t n -> p n t"))
-        size_flat = size_row[:].rearrange("p n t -> p (n t)")
+        key_scales = sb.tile([P, I], U8, align_bytes=64)
+        nc.vector.tensor_copy(key_scales[:], key_scale_pool[:].indirect(token_list[:]))
+        nc.vector.quantize_mx(
+            out=query_codes[:].bitcast(FP8X4), scales=query_scales[:], in_=query_bf[:].rearrange("p w j -> p (w j)")
+        )
 
         base = sb.tile([P, 3], F32)
         nc.gpsimd.memset(base[:, 2:3], GRAD_SCALE)
@@ -104,13 +102,8 @@ def tile_attend_blinked_s_kernel(
 
         key_codes = sb.tile([P, I], U32, align_bytes=64, tag="key_codes_then_gout_bf")
         score_ps = [ps.tile([P, HALF], F32, name=f"score_ps{h}") for h in range(2)]
-        nc.vector.tensor_copy(key_codes[:], key_pool[:].bitcast(U32).indirect(token_list[:]))
-        nc.vector.quantize_mx(
-            out=query_codes[:].bitcast(FP8X4), scales=query_scales[:], in_=query_bf[:].rearrange("p w j -> p (w j)")
-        )
-        key_scales = sb.tile([P, I], U8, align_bytes=64, tag="keys_then_scales")
         for h in range(2):
-            nc.vector.tensor_copy(key_scales[:, halves[h]], key_scale_pool[:].indirect(token_list[:, list_halves[h]]))
+            nc.vector.tensor_copy(key_codes[:, halves[h]], key_pool[:].bitcast(U32).indirect(token_list[:, list_halves[h]]))
             nc.tensor.matmul_mx(
                 out=score_ps[h][:],
                 lhsT=query_codes[:].bitcast(FP8X4),
@@ -124,19 +117,24 @@ def tile_attend_blinked_s_kernel(
 
         gout_bf = sb.tile([P, Q, PACK], BF16, align_bytes=64, tag="key_codes_then_gout_bf")
         nc.scalar.copy(gout_bf[:], gout_raw[:].rearrange("p j w -> p w j"))
-        gout_codes = sb.tile([P, Q], U32, align_bytes=64, tag="row_codes")
-        gout_scales = sb.tile([P, Q], U8, align_bytes=64, tag="row_scales")
-        val_codes = sb.tile([P, I], U32, align_bytes=64, tag="key_scales_then_val_codes")
-        nc.vector.tensor_copy(val_codes[:], val_pool[:].bitcast(U32).indirect(token_list[:]))
-        old_sb = late.tile([P, T], F32, align_bytes=64, tag="vals_then_old", offset=2112)
-        nc.sync.dma_start(out=old_sb[:], in_=old)
+
+        size_ps = ps.tile([P, PACK, P], F32)
+        for t in range(PACK):
+            nc.tensor.transpose(size_ps[:, t, :], size_cols[:, t : t + 1].to_broadcast([P, P]), ident[:])
+        size_row = sb.tile([P, P, PACK], F32)
+        nc.scalar.copy(size_row[:], size_ps[:].rearrange("p t n -> p n t"))
+        size_flat = size_row[:].rearrange("p n t -> p (n t)")
 
         linked = sb.tile([P, I], F32)
         nc.vector.tensor_copy(linked[:], sig[:].indirect(link_list[:]))
+        val_codes = sb.tile([P, I], U32, align_bytes=64, tag="sig_then_val_codes")
+        nc.vector.tensor_copy(val_codes[:], val_pool[:].bitcast(U32).indirect(token_list[:]))
+        val_scales = late.tile([P, I], U8, align_bytes=64, offset=10304)
+        gout_codes = late.tile([P, Q], U32, align_bytes=64, offset=10816)
+        gout_scales = late.tile([P, Q], U8, align_bytes=64, offset=11328)
         nc.vector.quantize_mx(
             out=gout_codes[:].bitcast(FP8X4), scales=gout_scales[:], in_=gout_bf[:].rearrange("p w j -> p (w j)")
         )
-        val_scales = sb.tile([P, I], U8, align_bytes=64, tag="sig_then_val_scales")
         dot_ps = [ps.tile([P, HALF], F32, name=f"dot_ps{h}") for h in range(2)]
         weighted = sb.tile([P, I], F32)
 
@@ -164,20 +162,22 @@ def tile_attend_blinked_s_kernel(
         row_sum = sb.tile([P, 1], F32)
         nc.scalar.activation(expo[:], logits[:], ACT.Exp, bias=neg_max[:], accum_out=row_sum[:])
         value_dots(1)
+        old_sb = late.tile([P, T], F32, offset=0)
+        nc.sync.dma_start(out=old_sb[:], in_=old)
+        inv_sum = sb.tile([P, 1], F32)
+        nc.vector.reciprocal(inv_sum[:], row_sum[:])
+        coef = sb.tile([P, 3], F32)
+        nc.vector.tensor_scalar(coef[:], base[:], inv_sum[:], None, ALU.mult)
         for h in range(2):
             nc.vector.tensor_tensor(weighted[:, halves[h]], dot_ps[h][:], size_flat[:, halves[h]], ALU.mult)
 
         nc.scalar.activation(logits[:], linked[:], ACT.Square, bias=-0.5)
 
-        inv_sum = sb.tile([P, 1], F32)
-        nc.vector.reciprocal(inv_sum[:], row_sum[:])
         products = sb.tile([P, I], F32)
         mean = sb.tile([P, 1], F32)
         nc.vector.scalar_tensor_tensor(
             products[:], expo[:], inv_sum[:], weighted[:], ALU.mult, ALU.mult, accum_out=mean[:]
         )
-        coef = sb.tile([P, 3], F32)
-        nc.vector.tensor_scalar(coef[:], base[:], inv_sum[:], None, ALU.mult)
         raw_grad = sb.tile([P, I], F32)
         nc.vector.scalar_tensor_tensor(raw_grad[:], weighted[:], mean[:], expo[:], ALU.subtract, ALU.mult)
         link_factor = sb.tile([P, I], F32)

@@ -21,7 +21,6 @@ P = 128
 PACK = 4
 HALF = I // 2
 SLOT_WINDOW = 704
-SIG_SPARE = 560
 GRAD_SCALE = 512.0
 STORE_WIDTHS = (256, 512, 512, 512, 256)
 
@@ -30,9 +29,9 @@ def load_words(nc, tile, words):
     nc.sync.dma_start(out=tile[:], in_=words[0].rearrange("p n t -> p (n t)").bitcast(I32))
 
 
-def load_scale_rows(queue, tile, scales):
+def load_scale_rows(nc, tile, scales):
     for quad in range(4):
-        queue.dma_start(
+        nc.scalar.dma_start(
             out=tile[32 * quad : 32 * quad + 4, :].bitcast(I32),
             in_=scales[0, 4 * quad : 4 * quad + 4, :].bitcast(I32),
         )
@@ -51,56 +50,68 @@ def tile_attend_blinked_s_kernel(
 
         token_list = sb.tile([P, I // 16], U16)
         link_list = sb.tile([P, I // 16], U16)
-        key_scale_pool = sb.tile([P, T], U8, align_bytes=64)
-        query_raw = sb.tile([P, PACK, Q], F32)
         key_pool = sb.tile([P, T], I32, align_bytes=64)
+        val_pool = sb.tile([P, T], I32, align_bytes=64, tag="vals_then_old")
+        key_scale_pool = sb.tile([P, T], U8, align_bytes=64)
+        val_scale_pool = sb.tile([P, T], U8, align_bytes=64)
+        query_raw = sb.tile([P, PACK, Q], F32)
+        gout_raw = sb.tile([P, PACK, Q], F32)
+        lam_col = sb.tile([P, 1], F32)
+        size_cols = sb.tile([P, PACK], F32)
+
         nc.vector.memset(key_scale_pool[:].bitcast(I32), 0)
+        nc.vector.memset(val_scale_pool[:].bitcast(I32), 0)
+        spare_in = sb.tile([P, SLOT_WINDOW - I], F32)
+        nc.vector.memset(spare_in[:], 0.0)
+
         nc.sync.dma_start(out=token_list[:], in_=offs)
-        nc.sync.dma_start(out=link_list[:], in_=offs2)
         nc.sync.dma_start(out=query_raw[:], in_=query.rearrange("(p j) w -> p j w", j=PACK))
+        load_scale_rows(nc, key_scale_pool, keys_scales)
         load_words(nc, key_pool, keys_words)
-        load_scale_rows(nc.scalar, key_scale_pool, keys_scales)
+        load_scale_rows(nc, val_scale_pool, vals_scales)
+        nc.scalar.dma_start(out=size_cols[:], in_=size.rearrange("o (p t) -> p (o t)", t=PACK))
+        nc.scalar.dma_start(out=lam_col[:], in_=lam)
+        nc.sync.dma_start(out=gout_raw[:], in_=gout.rearrange("(p j) w -> p j w", j=PACK))
+        nc.sync.dma_start(out=link_list[:], in_=offs2)
+        load_words(nc, val_pool, vals_words)
+
+        sig = sb.tile([P, SLOT_WINDOW], F32)
+        nc.scalar.activation(sig[:, I:], spare_in[:], ACT.Sigmoid)
+        link_grad = sb.tile([P, SLOT_WINDOW], F32)
+        token_grad = sb.tile([P, T], F32)
+        nc.vector.memset(token_grad[:], 0.0)
 
         ident = sb.tile([P, P], F32)
         make_identity(nc, ident[:])
 
-        sig = sb.tile([P, I + SIG_SPARE], F32, align_bytes=64, tag="sig_then_val_codes")
-        late = ctx.enter_context(tc.tile_pool(name="late", bufs=1))
-        spare_in = late.tile([P, SIG_SPARE], F32, offset=8128)
-        nc.vector.memset(spare_in[:], 0.0)
-        nc.scalar.activation(sig[:, I:], spare_in[:], ACT.Sigmoid)
-        val_scale_pool = late.tile([P, T], U8, align_bytes=64, offset=6144)
-        lam_col = late.tile([P, 1], F32, offset=8192)
-        size_cols = late.tile([P, PACK], F32, offset=8224)
-        gout_raw = late.tile([P, PACK, Q], F32, offset=8256)
-        val_pool = late.tile([P, T], I32, align_bytes=64, offset=10304)
-        load_words(nc, val_pool, vals_words)
-        nc.sync.dma_start(out=gout_raw[:], in_=gout.rearrange("(p j) w -> p j w", j=PACK))
-        nc.sync.dma_start(out=lam_col[:], in_=lam)
-        nc.sync.dma_start(out=size_cols[:], in_=size.rearrange("o (p t) -> p (o t)", t=PACK))
-
-        token_grad = sb.tile([P, T], F32)
-        nc.vector.memset(token_grad[:], 0.0)
-        link_grad = sb.tile([P, SLOT_WINDOW], F32)
-        nc.vector.memset(val_scale_pool[:].bitcast(I32), 0)
-        load_scale_rows(nc.sync, val_scale_pool, vals_scales)
-
         query_bf = sb.tile([P, Q, PACK], BF16, align_bytes=64)
         query_codes = sb.tile([P, Q], U32, align_bytes=64)
         query_scales = sb.tile([P, Q], U8, align_bytes=64)
-        nc.scalar.copy(query_bf[:], query_raw[:].rearrange("p j w -> p w j"))
+        nc.vector.tensor_copy(out=query_bf[:], in_=query_raw[:].rearrange("p j w -> p w j"))
         key_scales = sb.tile([P, I], U8, align_bytes=64)
         nc.vector.tensor_copy(key_scales[:], key_scale_pool[:].indirect(token_list[:]))
         nc.vector.quantize_mx(
             out=query_codes[:].bitcast(FP8X4), scales=query_scales[:], in_=query_bf[:].rearrange("p w j -> p (w j)")
         )
 
+        size_ps = ps.tile([P, PACK, P], F32)
+        for t in range(PACK):
+            nc.tensor.transpose(size_ps[:, t, :], size_cols[:, t : t + 1].to_broadcast([P, P]), ident[:])
+        size_row = sb.tile([P, P, PACK], F32)
+        nc.scalar.copy(size_row[:], size_ps[:].rearrange("p t n -> p n t"))
+        size_flat = size_row[:].rearrange("p n t -> p (n t)")
+
+        gout_bf = sb.tile([P, Q, PACK], BF16, align_bytes=64)
+        gout_codes = sb.tile([P, Q], U32, align_bytes=64)
+        gout_scales = sb.tile([P, Q], U8, align_bytes=64)
+        nc.scalar.copy(gout_bf[:], gout_raw[:].rearrange("p j w -> p w j"))
+
         base = sb.tile([P, 3], F32)
         nc.gpsimd.memset(base[:, 2:3], GRAD_SCALE)
         nc.gpsimd.tensor_scalar(base[:, 0:1], lam_col[:], -GRAD_SCALE, 0.0, ALU.mult, ALU.add)
         nc.gpsimd.tensor_scalar(base[:, 1:2], lam_col[:], GRAD_SCALE / 4, 0.0, ALU.mult, ALU.add)
 
-        key_codes = sb.tile([P, I], U32, align_bytes=64, tag="key_codes_then_gout_bf")
+        key_codes = sb.tile([P, I], U32, align_bytes=64)
         score_ps = [ps.tile([P, HALF], F32, name=f"score_ps{h}") for h in range(2)]
         for h in range(2):
             nc.vector.tensor_copy(key_codes[:, halves[h]], key_pool[:].bitcast(U32).indirect(token_list[:, list_halves[h]]))
@@ -115,31 +126,26 @@ def tile_attend_blinked_s_kernel(
             )
             nc.scalar.activation(sig[:, halves[h]], score_ps[h][:], ACT.Sigmoid)
 
-        gout_bf = sb.tile([P, Q, PACK], BF16, align_bytes=64, tag="key_codes_then_gout_bf")
-        nc.scalar.copy(gout_bf[:], gout_raw[:].rearrange("p j w -> p w j"))
-
-        size_ps = ps.tile([P, PACK, P], F32)
-        for t in range(PACK):
-            nc.tensor.transpose(size_ps[:, t, :], size_cols[:, t : t + 1].to_broadcast([P, P]), ident[:])
-        size_row = sb.tile([P, P, PACK], F32)
-        nc.scalar.copy(size_row[:], size_ps[:].rearrange("p t n -> p n t"))
-        size_flat = size_row[:].rearrange("p n t -> p (n t)")
-
-        linked = sb.tile([P, I], F32)
-        nc.vector.tensor_copy(linked[:], sig[:].indirect(link_list[:]))
-        val_codes = sb.tile([P, I], U32, align_bytes=64, tag="sig_then_val_codes")
-        nc.vector.tensor_copy(val_codes[:], val_pool[:].bitcast(U32).indirect(token_list[:]))
-        val_scales = late.tile([P, I], U8, align_bytes=64, offset=10304)
-        gout_codes = late.tile([P, Q], U32, align_bytes=64, offset=10816)
-        gout_scales = late.tile([P, Q], U8, align_bytes=64, offset=11328)
+        val_scales = sb.tile([P, I], U8, align_bytes=64)
+        nc.vector.tensor_copy(val_scales[:], val_scale_pool[:].indirect(token_list[:]))
         nc.vector.quantize_mx(
             out=gout_codes[:].bitcast(FP8X4), scales=gout_scales[:], in_=gout_bf[:].rearrange("p w j -> p (w j)")
         )
+
+        linked = sb.tile([P, I], F32)
+        nc.vector.tensor_copy(linked[:], sig[:].indirect(link_list[:]))
+        logits = sb.tile([P, I], F32)
+        for h in range(2):
+            nc.vector.scalar_tensor_tensor(
+                logits[:, halves[h]], linked[:, halves[h]], lam_col[:], score_ps[h][:], ALU.mult, ALU.add
+            )
+
+        val_codes = sb.tile([P, I], U32, align_bytes=64)
         dot_ps = [ps.tile([P, HALF], F32, name=f"dot_ps{h}") for h in range(2)]
         weighted = sb.tile([P, I], F32)
 
-        def value_dots(h):
-            nc.vector.tensor_copy(val_scales[:, halves[h]], val_scale_pool[:].indirect(token_list[:, list_halves[h]]))
+        def gather_values(h):
+            nc.vector.tensor_copy(val_codes[:, halves[h]], val_pool[:].bitcast(U32).indirect(token_list[:, list_halves[h]]))
             nc.tensor.matmul_mx(
                 out=dot_ps[h][:],
                 lhsT=gout_codes[:].bitcast(FP8X4),
@@ -150,19 +156,14 @@ def tile_attend_blinked_s_kernel(
                 stop=True,
             )
 
-        value_dots(0)
-        logits = sb.tile([P, I], F32)
-        for h in range(2):
-            nc.vector.scalar_tensor_tensor(
-                logits[:, halves[h]], linked[:, halves[h]], lam_col[:], score_ps[h][:], ALU.mult, ALU.add
-            )
+        gather_values(0)
         neg_max = sb.tile([P, 1], F32)
         nc.vector.tensor_reduce(neg_max[:], logits[:], AXIS.X, ALU.max, negate=True)
         expo = sb.tile([P, I], F32)
         row_sum = sb.tile([P, 1], F32)
         nc.scalar.activation(expo[:], logits[:], ACT.Exp, bias=neg_max[:], accum_out=row_sum[:])
-        value_dots(1)
-        old_sb = late.tile([P, T], F32, offset=0)
+        gather_values(1)
+        old_sb = sb.tile([P, T], F32, align_bytes=64, tag="vals_then_old")
         nc.sync.dma_start(out=old_sb[:], in_=old)
         inv_sum = sb.tile([P, 1], F32)
         nc.vector.reciprocal(inv_sum[:], row_sum[:])

@@ -112,7 +112,7 @@ def tile_attend_blinked_s_kernel(
         nc.gpsimd.tensor_scalar(base[:, 1:2], lam_col[:], GRAD_SCALE / 4, 0.0, ALU.mult, ALU.add)
 
         key_codes = sb.tile([P, I], U32, align_bytes=64)
-        score_ps = [ps.tile([P, HALF], F32, name=f"score_ps{h}") for h in range(2)]
+        score_ps = [ps.tile([P, HALF], F32, name=f"score_ps{h}", tag=f"bank{h}") for h in range(2)]
         for h in range(2):
             nc.vector.tensor_copy(key_codes[:, halves[h]], key_pool[:].bitcast(U32).indirect(token_list[:, list_halves[h]]))
             nc.tensor.matmul_mx(
@@ -141,7 +141,7 @@ def tile_attend_blinked_s_kernel(
             )
 
         val_codes = sb.tile([P, I], U32, align_bytes=64)
-        dot_ps = [ps.tile([P, HALF], F32, name=f"dot_ps{h}") for h in range(2)]
+        dot_ps = [ps.tile([P, HALF], F32, name=f"dot_ps{h}", tag=f"bank{h}") for h in range(2)]
         weighted = sb.tile([P, I], F32)
 
         def gather_values(h):
@@ -165,20 +165,20 @@ def tile_attend_blinked_s_kernel(
         gather_values(1)
         old_sb = sb.tile([P, T], F32, align_bytes=64, tag="vals_then_old")
         nc.sync.dma_start(out=old_sb[:], in_=old)
-        inv_sum = sb.tile([P, 1], F32)
-        nc.vector.reciprocal(inv_sum[:], row_sum[:])
-        coef = sb.tile([P, 3], F32)
-        nc.vector.tensor_scalar(coef[:], base[:], inv_sum[:], None, ALU.mult)
         for h in range(2):
             nc.vector.tensor_tensor(weighted[:, halves[h]], dot_ps[h][:], size_flat[:, halves[h]], ALU.mult)
 
         nc.scalar.activation(logits[:], linked[:], ACT.Square, bias=-0.5)
 
+        inv_sum = sb.tile([P, 1], F32)
+        nc.vector.reciprocal(inv_sum[:], row_sum[:])
         products = sb.tile([P, I], F32)
         mean = sb.tile([P, 1], F32)
         nc.vector.scalar_tensor_tensor(
             products[:], expo[:], inv_sum[:], weighted[:], ALU.mult, ALU.mult, accum_out=mean[:]
         )
+        coef = sb.tile([P, 3], F32)
+        nc.vector.tensor_scalar(coef[:], base[:], inv_sum[:], None, ALU.mult)
         raw_grad = sb.tile([P, I], F32)
         nc.vector.scalar_tensor_tensor(raw_grad[:], weighted[:], mean[:], expo[:], ALU.subtract, ALU.mult)
         link_factor = sb.tile([P, I], F32)

from contextlib import ExitStack

import concourse.mybir as mybir
from concourse.masks import make_identity

D, E, T, I, Q = 512, 512, 2048, 512, 128
FLOPS = 2 * Q * I * (D + E)

F32 = mybir.dt.float32
BF16 = mybir.dt.bfloat16
I32 = mybir.dt.int32
U32 = mybir.dt.uint32
U16 = mybir.dt.uint16
U8 = mybir.dt.uint8
FP8X4 = mybir.dt.float8_e4m3fn_x4
ALU = mybir.AluOpType
ACT = mybir.ActivationFunctionType
AXIS = mybir.AxisListType

P = 128
PACK = 4
HALF = I // 2
SLOT_WINDOW = 704
GRAD_SCALE = 512.0
STORE_WIDTHS = (256, 512, 512, 512, 256)


def load_words(nc, tile, words):
    nc.sync.dma_start(out=tile[:], in_=words[0].rearrange("p n t -> p (n t)").bitcast(I32))


def load_scale_rows(nc, tile, scales):
    for quad in range(4):
        nc.scalar.dma_start(
            out=tile[32 * quad : 32 * quad + 4, :].bitcast(I32),
            in_=scales[0, 4 * quad : 4 * quad + 4, :].bitcast(I32),
        )


def tile_attend_blinked_s_kernel(
    tc, query, lam, keys_words, keys_scales, gout, vals_words, vals_scales, size, old, offs, offs2, out
):
    nc = tc.nc
    halves = [slice(h * HALF, (h + 1) * HALF) for h in range(2)]
    list_halves = [slice(h * HALF // 16, (h + 1) * HALF // 16) for h in range(2)]

    with ExitStack() as ctx:
        sb = ctx.enter_context(tc.tile_pool(name="sb", bufs=1))
        ps = ctx.enter_context(tc.psum_pool(name="ps", bufs=1))

        token_list = sb.tile([P, I // 16], U16)
        link_list = sb.tile([P, I // 16], U16)
        key_pool = sb.tile([P, T], I32, align_bytes=64)
        val_pool = sb.tile([P, T], I32, align_bytes=64, tag="vals_then_old")
        key_scale_pool = sb.tile([P, T], U8, align_bytes=64)
        val_scale_pool = sb.tile([P, T], U8, align_bytes=64)
        query_raw = sb.tile([P, PACK, Q], F32)
        gout_raw = sb.tile([P, PACK, Q], F32)
        lam_col = sb.tile([P, 1], F32)
        size_cols = sb.tile([P, PACK], F32)

        nc.vector.memset(key_scale_pool[:].bitcast(I32), 0)
        nc.vector.memset(val_scale_pool[:].bitcast(I32), 0)
        spare_in = sb.tile([P, SLOT_WINDOW - I], F32)
        nc.vector.memset(spare_in[:], 0.0)

        nc.sync.dma_start(out=token_list[:], in_=offs)
        nc.sync.dma_start(out=query_raw[:], in_=query.rearrange("(p j) w -> p j w", j=PACK))
        load_scale_rows(nc, key_scale_pool, keys_scales)
        load_words(nc, key_pool, keys_words)
        load_scale_rows(nc, val_scale_pool, vals_scales)
        nc.scalar.dma_start(out=size_cols[:], in_=size.rearrange("o (p t) -> p (o t)", t=PACK))
        nc.scalar.dma_start(out=lam_col[:], in_=lam)
        nc.sync.dma_start(out=gout_raw[:], in_=gout.rearrange("(p j) w -> p j w", j=PACK))
        nc.sync.dma_start(out=link_list[:], in_=offs2)
        load_words(nc, val_pool, vals_words)

        sig = sb.tile([P, SLOT_WINDOW], F32)
        nc.scalar.activation(sig[:, I:], spare_in[:], ACT.Sigmoid)
        link_grad = sb.tile([P, SLOT_WINDOW], F32)
        token_grad = sb.tile([P, T], F32)
        nc.vector.memset(token_grad[:], 0.0)

        ident = sb.tile([P, P], F32)
        make_identity(nc, ident[:])

        query_bf = sb.tile([P, Q, PACK], BF16, align_bytes=64)
        query_codes = sb.tile([P, Q], U32, align_bytes=64)
        query_scales = sb.tile([P, Q], U8, align_bytes=64)
        nc.vector.tensor_copy(out=query_bf[:], in_=query_raw[:].rearrange("p j w -> p w j"))
        key_scales = sb.tile([P, I], U8, align_bytes=64)
        nc.vector.tensor_copy(key_scales[:], key_scale_pool[:].indirect(token_list[:]))
        nc.vector.quantize_mx(
            out=query_codes[:].bitcast(FP8X4), scales=query_scales[:], in_=query_bf[:].rearrange("p w j -> p (w j)")
        )

        size_ps = ps.tile([P, PACK, P], F32)
        for t in range(PACK):
            nc.tensor.transpose(size_ps[:, t, :], size_cols[:, t : t + 1].to_broadcast([P, P]), ident[:])
        size_row = sb.tile([P, P, PACK], F32)
        nc.scalar.copy(size_row[:], size_ps[:].rearrange("p t n -> p n t"))
        size_flat = size_row[:].rearrange("p n t -> p (n t)")

        gout_bf = sb.tile([P, Q, PACK], BF16, align_bytes=64)
        gout_codes = sb.tile([P, Q], U32, align_bytes=64)
        gout_scales = sb.tile([P, Q], U8, align_bytes=64)
        nc.scalar.copy(gout_bf[:], gout_raw[:].rearrange("p j w -> p w j"))

        base = sb.tile([P, 3], F32)
        nc.gpsimd.memset(base[:, 2:3], GRAD_SCALE)
        nc.gpsimd.tensor_scalar(base[:, 0:1], lam_col[:], -GRAD_SCALE, 0.0, ALU.mult, ALU.add)
        nc.gpsimd.tensor_scalar(base[:, 1:2], lam_col[:], GRAD_SCALE / 4, 0.0, ALU.mult, ALU.add)

        key_codes = sb.tile([P, I], U32, align_bytes=64)
        score_ps = [ps.tile([P, HALF], F32, name=f"score_ps{h}", tag=f"bank{h}") for h in range(2)]
        for h in range(2):
            nc.vector.tensor_copy(key_codes[:, halves[h]], key_pool[:].bitcast(U32).indirect(token_list[:, list_halves[h]]))
            nc.tensor.matmul_mx(
                out=score_ps[h][:],
                lhsT=query_codes[:].bitcast(FP8X4),
                lhsT_scale=query_scales[:],
                rhs=key_codes[:, halves[h]].bitcast(FP8X4),
                rhs_scale=key_scales[:, halves[h]],
                start=True,
                stop=True,
            )
            nc.scalar.activation(sig[:, halves[h]], score_ps[h][:], ACT.Sigmoid)

        val_scales = sb.tile([P, I], U8, align_bytes=64)
        nc.vector.tensor_copy(val_scales[:], val_scale_pool[:].indirect(token_list[:]))
        nc.vector.quantize_mx(
            out=gout_codes[:].bitcast(FP8X4), scales=gout_scales[:], in_=gout_bf[:].rearrange("p w j -> p (w j)")
        )

        linked = sb.tile([P, I], F32)
        nc.vector.tensor_copy(linked[:], sig[:].indirect(link_list[:]))
        logits = sb.tile([P, I], F32)
        for h in range(2):
            nc.vector.scalar_tensor_tensor(
                logits[:, halves[h]], linked[:, halves[h]], lam_col[:], score_ps[h][:], ALU.mult, ALU.add
            )

        val_codes = sb.tile([P, I], U32, align_bytes=64)
        dot_ps = [ps.tile([P, HALF], F32, name=f"dot_ps{h}", tag=f"bank{h}") for h in range(2)]
        weighted = sb.tile([P, I], F32)

        def gather_values(h):
            nc.vector.tensor_copy(val_codes[:, halves[h]], val_pool[:].bitcast(U32).indirect(token_list[:, list_halves[h]]))
            nc.tensor.matmul_mx(
                out=dot_ps[h][:],
                lhsT=gout_codes[:].bitcast(FP8X4),
                lhsT_scale=gout_scales[:],
                rhs=val_codes[:, halves[h]].bitcast(FP8X4),
                rhs_scale=val_scales[:, halves[h]],
                start=True,
                stop=True,
            )

        gather_values(0)
        neg_max = sb.tile([P, 1], F32)
        nc.vector.tensor_reduce(neg_max[:], logits[:], AXIS.X, ALU.max, negate=True)
        expo = sb.tile([P, I], F32)
        row_sum = sb.tile([P, 1], F32)
        nc.scalar.activation(expo[:], logits[:], ACT.Exp, bias=neg_max[:], accum_out=row_sum[:])
        gather_values(1)
        old_sb = sb.tile([P, T], F32, align_bytes=64, tag="vals_then_old")
        nc.sync.dma_start(out=old_sb[:], in_=old)
        for h in range(2):
            nc.vector.tensor_tensor(weighted[:, halves[h]], dot_ps[h][:], size_flat[:, halves[h]], ALU.mult)

        nc.scalar.activation(logits[:], linked[:], ACT.Square, bias=-0.5)

        inv_sum = sb.tile([P, 1], F32)
        nc.vector.reciprocal(inv_sum[:], row_sum[:])
        products = sb.tile([P, I], F32)
        mean = sb.tile([P, 1], F32)
        nc.vector.scalar_tensor_tensor(
            products[:], expo[:], inv_sum[:], weighted[:], ALU.mult, ALU.mult, accum_out=mean[:]
        )
        coef = sb.tile([P, 3], F32)
        nc.vector.tensor_scalar(coef[:], base[:], inv_sum[:], None, ALU.mult)
        raw_grad = sb.tile([P, I], F32)
        nc.vector.scalar_tensor_tensor(raw_grad[:], weighted[:], mean[:], expo[:], ALU.subtract, ALU.mult)
        link_factor = sb.tile([P, I], F32)
        nc.scalar.activation(link_factor[:], logits[:], ACT.Identity, bias=coef[:, 1:2], scale=coef[:, 0:1])
        nc.vector.tensor_tensor(link_grad[:].indirect(link_list[:]), raw_grad[:], link_factor[:], ALU.mult)
        own_grad = sb.tile([P, I], F32)
        nc.scalar.activation(own_grad[:], raw_grad[:], ACT.Copy, scale=coef[:, 2:3])
        nc.vector.tensor_tensor(token_grad[:].indirect(token_list[:]), link_grad[:, :I], own_grad[:], ALU.add)

        start = 0
        for n, width in enumerate(STORE_WIDTHS):
            cols = slice(start, start + width)
            result = sb.tile([P, width], F32, name=f"result{n}")
            nc.vector.tensor_tensor(result[:], old_sb[:, cols], token_grad[:, cols], ALU.add)
            queue = nc.sync if n % 2 == 0 else nc.scalar
            queue.dma_start(out=out[:, cols], in_=result[:])
            start = start + width
